import numpy as np
import ml_dtypes


def mxq(x, axis, fmt="e4m3"):
    dtype, down = {"e4m3": (ml_dtypes.float8_e4m3fn, 7), "e5m2": (ml_dtypes.float8_e5m2, 14)}[fmt]
    v = np.moveaxis(np.asarray(x, np.float32).astype(ml_dtypes.bfloat16).astype(np.float64), axis, -1)
    blocks = v.reshape(v.shape[:-1] + (-1, 32))
    amax = np.abs(blocks).max(-1, keepdims=True)
    byte = np.maximum(np.where(amax > 0, np.frexp(amax)[1] - 1 + 127, 0) - down, 1)
    scale = np.exp2(byte - 127.0)
    codes = (blocks / scale).astype(np.float32).astype(dtype).astype(np.float64)
    return np.moveaxis((codes * scale).reshape(v.shape), -1, axis)


WIDE = False


def mx_kscale(k):
    if not WIDE:
        return np.ones(k)
    levels = np.array([10, -10, 5, -5, 0])
    if k % 512:
        return np.exp2(np.random.permutation(np.resize(levels, k // 32))).repeat(32)
    a = np.empty((k // 512, 16))
    for p in range(k // 512):
        a[p, :8] = np.random.permutation(np.resize(levels, 8))
        for g in range(8):
            far = levels[np.abs(levels - a[p, g]) >= 10]
            a[p, g + 8] = far[np.random.randint(len(far))]
    return np.exp2(a.ravel()).repeat(32)


def f64(x):
    return np.asarray(x).astype(np.float64)


def striped(idx):
    return np.tile(idx.reshape(-1, 16).T, (8, 1)).astype(np.uint16)


def unstriped(offs):
    return offs[:16].T.reshape(-1).astype(np.int64)


E2M1 = np.array([0.0, 0.5, 1.0, 1.5, 2.0, 3.0, 4.0, 6.0, -0.0, -0.5, -1.0, -1.5, -2.0, -3.0, -4.0, -6.0])


def pack_weight(w, fmt):
    k, n = w.shape
    w = f64(np.asarray(w, np.float32).astype(ml_dtypes.bfloat16)).reshape(k // 32, 32, n)
    amax = np.abs(w).max(1)
    if fmt == "e4m3":
        byte = np.frexp(amax)[1] - 1 + 127 - 7
    else:
        mant, ex = np.frexp(amax / 6.0)
        byte = np.where(mant > 0.5, ex, ex - 1) + 127
    byte = np.clip(np.where(amax > 0, byte, 1), 1, 254)
    scaled = (w * np.exp2(127.0 - byte)[:, None, :]).reshape(k, n).astype(np.float32)
    by_word = np.ascontiguousarray(scaled.reshape(k // 512, 128, 4, n).transpose(0, 1, 3, 2))
    if fmt == "e4m3":
        words = by_word.astype(ml_dtypes.float8_e4m3fn).view(np.uint8)
    else:
        c = by_word.astype(ml_dtypes.float4_e2m1fn).view(np.uint8) & 0xF
        words = (c[..., 0::2] | (c[..., 1::2] << 4)).reshape(k // 512, 128, 2 * n)
    return np.ascontiguousarray(words), np.ascontiguousarray(byte.astype(np.uint8).reshape(k // 512, 16, n))


def unpack_weight(words, scales, fmt):
    g, _, n = scales.shape
    words = np.ascontiguousarray(words).reshape(g, 128, n, -1)
    if fmt == "e4m3":
        vals = words.view(ml_dtypes.float8_e4m3fn).astype(np.float64)
    else:
        nib = np.empty((g, 128, n, 4), np.uint8)
        nib[..., 0::2] = words & 0xF
        nib[..., 1::2] = words >> 4
        vals = E2M1[nib]
    vals = vals * np.repeat(np.exp2(scales.astype(np.float64) - 127.0), 8, axis=1)[..., None]
    return vals.transpose(0, 1, 3, 2).reshape(g * 512, n)


def gelu(v):
    return 0.5 * v * (1.0 + np.tanh(np.sqrt(2.0 / np.pi) * (v + 0.044715 * v**3)))


def bf(x):
    return np.asarray(x, np.float32).astype(ml_dtypes.bfloat16)


def planes(Y):
    n, m = Y.shape
    b = f64(bf(Y)).reshape(n // 32, 32, m)
    amax = np.abs(b).max(1)
    byte = np.clip(np.where(amax > 0, np.frexp(amax)[1] - 1 + 127 - 7, 1), 1, 254)
    codes = (b * np.exp2(127.0 - byte)[:, None, :]).reshape(n, m).astype(np.float32).astype(ml_dtypes.float8_e4m3fn).view(np.uint8)
    words = codes.reshape(n // 512, 128, 4, m).transpose(0, 1, 3, 2)
    return np.ascontiguousarray(words), np.ascontiguousarray(byte.astype(np.uint8).reshape(n // 512, 16, m))


K, T, S, H, T2, P, N = 1024, 2048, 1024, 512, 2048, 1024, 384


def setup_inputs():
    n = np.random.standard_normal
    s = mx_kscale(K)[:, None]
    u = mx_kscale(H)[:, None]
    d = {}
    d["tab_words"], d["tab_scales"] = pack_weight(n((K, T)) * s, "e4m3")
    d["offs"] = striped(np.random.permutation(T)[:S])
    d["offs2"] = striped(np.random.permutation(T2)[:S])
    d["offs3"] = striped(np.random.permutation(T2)[:P])
    d["w1"] = (1.5 * n((K, H)) / K ** 0.5 / s).astype(np.float32)
    d["w2_words"], d["w2_scales"] = pack_weight(1.2 * n((K, H)) / K ** 0.5 / s, "e2m1")
    d["gain"] = (np.exp(0.3 * n(H)) * u[:, 0]).astype(np.float32)
    d["page0"] = (n((H, T2)) * u).astype(np.float32)
    d["wgs"] = np.exp(0.3 * n((128, S))).astype(np.float32)
    d["base"] = (0.8 * n(H) * u[:, 0]).astype(np.float32)
    d["w3"] = (n((H, N)) / H ** 0.5 / u).astype(np.float32)
    d["w4_words"], d["w4_scales"] = pack_weight(n((H, N)) / H ** 0.5 / u, "e4m3")
    return d


def reference(tab_words, tab_scales, offs, offs2, offs3, w1, w2_words, w2_scales, gain, page0, wgs, base, w3, w4_words, w4_scales):
    v = unpack_weight(tab_words, tab_scales, "e4m3")[:, unstriped(offs)]
    a = mxq(f64(w1), 0, "e4m3").T @ v
    b = unpack_weight(w2_words, w2_scales, "e2m1").T @ v
    h = f64(gain)[:, None] * (a / (1.0 + b * b))
    page = f64(page0).copy()
    page[:, unstriped(offs2)] = np.tile(f64(wgs), (H // 128, 1)) * h
    x = page[:, unstriped(offs3)] - f64(base)[:, None]
    cells = mxq(f64(w3), 0, "e4m3").T @ mxq(x, 0, "e4m3")
    own = unpack_weight(w4_words, w4_scales, "e4m3").T @ mxq(h, 0, "e4m3")
    y = cells - own
    words, scales = planes(page)
    return y, page, words, scales

@@ -1,0 +1,319 @@
+from contextlib import ExitStack
+
+import concourse.mybir as mybir
+
+K, T, S, H, T2, N = 1024, 2048, 1024, 512, 2048, 384
+FLOPS = 2 * (2 * K * H * S + 2 * H * N * S)
+
+F32 = mybir.dt.float32
+BF16 = mybir.dt.bfloat16
+I32 = mybir.dt.int32
+U32 = mybir.dt.uint32
+U16 = mybir.dt.uint16
+U8 = mybir.dt.uint8
+FP8X4 = mybir.dt.float8_e4m3fn_x4
+FP4X4 = mybir.dt.float4_e2m1fn_x4
+ACT = mybir.ActivationFunctionType
+ALU = mybir.AluOpType
+
+P = 128
+PACK = 4
+QUAD = 32
+PASSES = K // (P * PACK)
+HALF = 512
+HALVES = S // HALF
+LIST_COLS = S // 16
+PAGE_CHUNK = 512
+
+
+def tile_list_glucose_hour_cells_kernel(
+    tc, tab_words, tab_scales, offs, offs2, offs3, w1, w2_words, w2_scales, gain, page0, wgs, base, w3,
+    w4_words, w4_scales, out_0, out_1, out_2, out_3,
+):
+    nc = tc.nc
+    with ExitStack() as ctx:
+        keep = ctx.enter_context(tc.tile_pool(name="keep", bufs=1))
+        work = ctx.enter_context(tc.tile_pool(name="work", bufs=4))
+        psum = ctx.enter_context(tc.psum_pool(name="psum", bufs=4))
+
+        def held(name, shape, dtype, tag=None):
+            return keep.tile(shape, dtype, name=name, tag=tag or name, align_bytes=64)
+
+        def half_cols(c):
+            return slice(c * HALF, (c + 1) * HALF)
+
+        def half_list(lst, c):
+            return lst[:, c * HALF // 16 : (c + 1) * HALF // 16]
+
+        def weave_out(flat):
+            return flat.rearrange("p (c i t) -> p c t i", i=4, t=PACK)
+
+        def weave_in(rows):
+            return rows.rearrange("p t (c i) -> p c t i", i=4)
+
+        pick = keep.tile([P, LIST_COLS], U16, name="pick")
+        put = keep.tile([P, LIST_COLS], U16, name="put")
+        read = keep.tile([P, LIST_COLS], U16, name="read")
+
+        tab_s = held("tab_s", [P, PASSES * T], U8)
+        w2_s_raw = held("w2_s_raw", [P, PASSES * H], U8)
+        w4_s = held("w4_s", [P, N], U8)
+        nc.vector.memset(tab_s[:].bitcast(I32), 0)
+        nc.gpsimd.memset(w2_s_raw[:].bitcast(I32), 0)
+        nc.gpsimd.memset(w4_s[:].bitcast(I32), 0)
+
+        warm = held("warm", [P, 1], F32)
+        warm_out = held("warm_out", [P, 1], F32)
+        nc.vector.memset(warm[:], 1.0)
+        nc.scalar.activation(warm_out[:], warm[:], ACT.Abs_reciprocal_sqrt)
+
+        tab_w = [held(f"tab_w{a}", [P, T], U32) for a in range(PASSES)]
+        w1_raw = [held(f"w1_raw{a}", [P, PACK, H], F32) for a in range(PASSES)]
+        w2_w_raw = held("w2_w_raw", [P, PASSES, 2 * H], U8)
+        gain_t = held("gain_t", [P, PACK], F32)
+        base_t = held("base_t", [P, PACK], F32)
+        page = [held(f"page{t}", [P, T2], F32) for t in range(PACK)]
+        wgs_t = [held(f"wgs{t}", [P, S], F32) for t in range(PACK)]
+        w3_raw = held("w3_raw", [P, PACK, N], F32)
+        w4_w = held("w4_w", [P, N], U32)
+        page0_rows = page0.rearrange("(p t) m -> p t m", t=PACK)
+        wgs_rows = wgs.rearrange("(q t) s -> q t s", t=PACK)
+
+        def load_tab(a):
+            nc.sync.dma_start(tab_w[a][:].bitcast(I32), tab_words[a].rearrange("p n i -> p (n i)").bitcast(I32))
+
+        def load_w1(a):
+            rows = w1[a * P * PACK : (a + 1) * P * PACK, :]
+            nc.sync.dma_start(w1_raw[a][:], rows.rearrange("(p j) c -> p j c", j=PACK))
+
+        def load_scales(queue, plane, scales):
+            for quad in (0, 2, 1, 3):
+                queue.dma_start(
+                    plane[quad * QUAD : quad * QUAD + 4, :].bitcast(I32).rearrange("r (a n) -> r a n", a=scales.shape[0]),
+                    scales[:, 4 * quad : 4 * quad + 4, :].rearrange("a r n -> r a n").bitcast(I32),
+                )
+
+        def load_slice(t):
+            nc.sync.dma_start(page[t][:], page0_rows[:, t, :])
+            for quad in (0, 2, 1, 3):
+                nc.sync.dma_start(wgs_t[t][quad * QUAD : (quad + 1) * QUAD, :], wgs_rows[:, t, :])
+
+        nc.sync.dma_start(w2_w_raw[:].bitcast(I32), w2_words.rearrange("a p n -> p a n").bitcast(I32))
+        nc.sync.dma_start(pick[:], offs)
+        nc.sync.dma_start(put[:], offs2)
+        load_scales(nc.sync, tab_s, tab_scales)
+        load_tab(0)
+        load_scales(nc.sync, w2_s_raw, w2_scales)
+        load_w1(0)
+        load_tab(1)
+        load_w1(1)
+        nc.sync.dma_start(gain_t[:], gain.rearrange("(p t) -> p t", t=PACK))
+        load_slice(0)
+        nc.sync.dma_start(read[:], offs3)
+        nc.sync.dma_start(base_t[:], base.rearrange("(p t) -> p t", t=PACK))
+        load_slice(1)
+        nc.sync.dma_start(w3_raw[:], w3.rearrange("(p j) n -> p j n", j=PACK))
+
+        w2_w = held("w2_w", [P, PASSES, 2 * H], U8)
+        w2_s = held("w2_s", [P, PASSES * H], U8)
+        for a in range(PASSES):
+            nc.vector.tensor_copy(
+                w2_w[:, a, :].rearrange("p (t q b) -> p t q b", t=PACK, b=2),
+                w2_w_raw[:, a, :].rearrange("p (q t b) -> p t q b", t=PACK, b=2),
+            )
+        v_s = [held(f"v_s{a}", [P, S], U8) for a in range(PASSES)]
+        v_w = [held(f"v_w{a}", [P, S], U32) for a in range(PASSES)]
+        for a in range(PASSES):
+            nc.vector.tensor_copy(v_s[a][:], tab_s[:, a * T : (a + 1) * T].indirect(pick[:]))
+        nc.vector.tensor_copy(v_w[0][:], tab_w[0][:].indirect(pick[:]))
+        nc.vector.tensor_copy(
+            w2_s[:].rearrange("p (a t q) -> p a t q", a=PASSES, t=PACK),
+            w2_s_raw[:].rearrange("p (a q t) -> p a t q", a=PASSES, t=PACK),
+        )
+        for c in range(HALVES):
+            nc.vector.tensor_copy(v_w[1][:, half_cols(c)], tab_w[1][:].indirect(half_list(pick, c)))
+
+        w1_b = [held(f"w1_b{a}", [P, PACK * H], BF16) for a in range(PASSES)]
+        w1_w = [held("w1_w0", [P, H], U32, "tab_w1"), held("w1_w1", [P, H], U32)]
+        w1_s = [held(f"w1_s{a}", [P, H], U8) for a in range(PASSES)]
+        for a in range(PASSES):
+            dst = w1_b[a][:].rearrange("p (t q j) -> p q j t", t=PACK, j=PACK)
+            src = w1_raw[a][:].rearrange("p j (q t) -> p q j t", t=PACK)
+            if a == 0:
+                nc.scalar.copy(dst, src)
+            else:
+                nc.vector.tensor_copy(dst, src)
+            nc.vector.quantize_mx(out=w1_w[a][:].bitcast(FP8X4), scales=w1_s[a][:], in_=w1_b[a][:])
+
+        h = held("h", [P, PACK, S], F32)
+        x_pairs = [held(f"x_pairs{c}", [P, 2, HALF, 2], BF16, f"w1_b{c}") for c in range(HALVES)]
+        y_pairs = [held(f"y_pairs{k}", [P, 2, PAGE_CHUNK, 2], BF16) for k in range(T2 // PAGE_CHUNK)]
+
+        def round_page(t, k):
+            nc.scalar.copy(y_pairs[k][:, t // 2, :, t % 2], page[t][:, k * PAGE_CHUNK : (k + 1) * PAGE_CHUNK])
+
+        def weave_pairs(pairs, copy, word):
+            woven = work.tile([P, PACK * HALF], BF16, name="woven", bufs=5, align_bytes=64)
+            copy(
+                woven[:].bitcast(word).rearrange("p (c i u) -> p c u i", i=4, u=2),
+                pairs[:].rearrange("p u m e -> p u (m e)").bitcast(word).rearrange("p u (c i) -> p c u i", i=4),
+            )
+            return woven
+
+        out_1_rows = out_1.rearrange("(p t) m -> p t m", t=PACK)
+
+        def root(t):
+            banks, sq, rs = [], [], []
+            for c in range(HALVES):
+                b_ps = psum.tile([P, HALF], F32, name="b_bank")
+                for a in range(PASSES):
+                    nc.tensor.matmul_mx(
+                        out=b_ps[:],
+                        lhsT=w2_w[:, a, 2 * t * P : 2 * (t + 1) * P].bitcast(FP4X4),
+                        lhsT_scale=w2_s[:, a * H + t * P : a * H + (t + 1) * P],
+                        rhs=v_w[a][:, half_cols(c)].bitcast(FP8X4),
+                        rhs_scale=v_s[a][:, half_cols(c)],
+                        start=(a == 0),
+                        stop=(a == PASSES - 1),
+                    )
+                banks.append(b_ps)
+            for c in range(HALVES):
+                sq.append(work.tile([P, HALF], F32, name="sq", bufs=2))
+                nc.scalar.activation(sq[c][:], banks[c][:], ACT.Square)
+            for c in range(HALVES):
+                rs.append(work.tile([P, HALF], F32, name="rs", bufs=8))
+                nc.scalar.activation(rs[c][:], sq[c][:], ACT.Abs_reciprocal_sqrt, bias=1.0)
+            return rs
+
+        def features(t, rs):
+            rows = slice(t * P, (t + 1) * P)
+            damp = held(f"damp{t}", [P, S], F32, f"wgs{t - 1}" if t else None)
+            for c in range(HALVES):
+                nc.scalar.activation(damp[:, half_cols(c)], rs[c][:], ACT.Square)
+            for c in range(HALVES):
+                a_ps = psum.tile([P, HALF], F32, name="a_bank")
+                for a in range(PASSES):
+                    nc.tensor.matmul_mx(
+                        out=a_ps[:],
+                        lhsT=w1_w[a][:, rows].bitcast(FP8X4),
+                        lhsT_scale=w1_s[a][:, rows],
+                        rhs=v_w[a][:, half_cols(c)].bitcast(FP8X4),
+                        rhs_scale=v_s[a][:, half_cols(c)],
+                        start=(a == 0),
+                        stop=(a == PASSES - 1),
+                    )
+                nc.vector.scalar_tensor_tensor(
+                    h[:, t, half_cols(c)], a_ps[:], gain_t[:, t : t + 1], damp[:, half_cols(c)], ALU.mult, ALU.mult
+                )
+
+        def scatter(t):
+            nc.vector.tensor_tensor(page[t][:].indirect(put[:]), h[:, t, :], wgs_t[t][:], ALU.mult)
+            nc.sync.dma_start(out_1_rows[:, t, :], page[t][:])
+
+        def fetch(t):
+            for c in range(HALVES):
+                round_page(t, c)
+                got = work.tile([P, HALF], F32, name="got", bufs=4)
+                nc.vector.tensor_copy(got[:], page[t][:].indirect(half_list(read, c)))
+                nc.scalar.activation(
+                    x_pairs[c][:, t // 2, :, t % 2], got[:], ACT.Identity, bias=base_t[:, t : t + 1], scale=-1.0
+                )
+            for k in range(HALVES, T2 // PAGE_CHUNK):
+                round_page(t, k)
+
+        roots = [root(0)]
+        features(0, roots[0])
+        roots.extend(root(t) for t in range(1, PACK))
+        for t in range(PACK - 1):
+            scatter(t)
+            if t + 2 < PACK:
+                load_slice(t + 2)
+            features(t + 1, roots[t + 1])
+            fetch(t)
+        nc.sync.dma_start(w4_w[:].bitcast(I32), w4_words[0].rearrange("p n i -> p (n i)").bitcast(I32))
+        load_scales(nc.sync, w4_s, w4_scales)
+
+        w3_b = held("w3_b", [P, PACK * N], BF16)
+        w3_w = held("w3_w", [P, N], U32, "wgs2")
+        w3_s = held("w3_s", [P, N], U8)
+        nc.scalar.copy(weave_out(w3_b[:]), weave_in(w3_raw[:]))
+        for lo, hi in ((0, 256), (256, N)):
+            nc.vector.quantize_mx(
+                out=w3_w[:, lo:hi].bitcast(FP8X4), scales=w3_s[:, lo:hi], in_=w3_b[:, PACK * lo : PACK * hi]
+            )
+
+        woven_h = []
+        for c in range(HALVES):
+            woven_h.append(work.tile([P, PACK * HALF], BF16, name="woven", bufs=5, align_bytes=64))
+            nc.scalar.copy(weave_out(woven_h[c][:]), weave_in(h[:, :, half_cols(c)]))
+
+        scatter(PACK - 1)
+        fetch(PACK - 1)
+
+        h_w = held("h_w", [P, S], U32, "wgs3")
+        h_s = held("h_s", [P, S], U8)
+        score = {}
+
+        def own_scores(c):
+            nc.vector.quantize_mx(
+                out=h_w[:, half_cols(c)].bitcast(FP8X4), scales=h_s[:, half_cols(c)], in_=woven_h[c][:]
+            )
+            for nb in range(N // P):
+                rows = slice(nb * P, (nb + 1) * P)
+                score[c, nb] = psum.tile([P, HALF], F32, name=("a_bank", "b_bank")[c])
+                nc.tensor.matmul_mx(
+                    out=score[c, nb][:],
+                    lhsT=w4_w[:, rows].bitcast(FP8X4),
+                    lhsT_scale=w4_s[:, rows],
+                    rhs=h_w[:, half_cols(c)].bitcast(FP8X4),
+                    rhs_scale=h_s[:, half_cols(c)],
+                    start=True,
+                    stop=False,
+                )
+
+        x_w = held("x_w", [P, S], U32, "tab_w1")
+        x_s = held("x_s", [P, S], U8)
+        y_w = held("y_w", [P, T2], U32, "tab_w0")
+        y_s = held("y_s", [P, T2], U8)
+        words_out = out_2[0].rearrange("p m i -> p (m i)").bitcast(I32)
+
+        def scores(c, woven):
+            nc.vector.quantize_mx(out=x_w[:, half_cols(c)].bitcast(FP8X4), scales=x_s[:, half_cols(c)], in_=woven[:])
+            for nb in range(N // P):
+                rows = slice(nb * P, (nb + 1) * P)
+                nc.tensor.matmul_mx(
+                    out=score[c, nb][:],
+                    lhsT=w3_w[:, rows].bitcast(FP8X4),
+                    lhsT_scale=w3_s[:, rows],
+                    rhs=x_w[:, half_cols(c)].bitcast(FP8X4),
+                    rhs_scale=x_s[:, half_cols(c)],
+                    start=False,
+                    stop=True,
+                )
+                y = work.tile([P, HALF], F32, name="y", tag="rs", bufs=8)
+                nc.scalar.activation(y[:], score[c, nb][:], ACT.Copy, scale=-1.0)
+                nc.sync.dma_start(out_0[rows, half_cols(c)], y[:])
+
+        def planes(k, woven):
+            cols = slice(k * PAGE_CHUNK, (k + 1) * PAGE_CHUNK)
+            nc.vector.quantize_mx(out=y_w[:, cols].bitcast(FP8X4), scales=y_s[:, cols], in_=woven[:])
+            nc.sync.dma_start(words_out[:, cols], y_w[:, cols].bitcast(I32))
+
+        own_scores(0)
+        wx0 = weave_pairs(x_pairs[0], nc.vector.tensor_copy, I32)
+        wy0 = weave_pairs(y_pairs[0], nc.vector.tensor_copy, I32)
+        scores(0, wx0)
+        planes(0, wy0)
+        own_scores(1)
+        wx1 = weave_pairs(x_pairs[1], nc.vector.tensor_copy, I32)
+        wy1 = weave_pairs(y_pairs[1], nc.vector.tensor_copy, I32)
+        scores(1, wx1)
+        planes(1, wy1)
+        wy2 = weave_pairs(y_pairs[2], nc.vector.tensor_copy, I32)
+        wy3 = weave_pairs(y_pairs[3], nc.vector.tensor_copy, I32)
+        planes(2, wy2)
+        planes(3, wy3)
+        for quad in range(4):
+            nc.sync.dma_start(
+                out_3[0, 4 * quad : 4 * quad + 4, :].bitcast(I32), y_s[quad * QUAD : quad * QUAD + 4, :].bitcast(I32)
+            )

@@ -55,12 +55,14 @@ def tile_list_glucose_hour_cells_kernel(
         put = keep.tile([P, LIST_COLS], U16, name="put")
         read = keep.tile([P, LIST_COLS], U16, name="read")
 
-        tab_s = held("tab_s", [P, PASSES * T], U8)
+        tab_s = held("tab_s", [P, T], U8)
+        v_s1 = held("v_s1", [P, S], U8)
         w2_s_raw = held("w2_s_raw", [P, PASSES * H], U8)
         w4_s = held("w4_s", [P, N], U8)
         nc.vector.memset(tab_s[:].bitcast(I32), 0)
         nc.gpsimd.memset(w2_s_raw[:].bitcast(I32), 0)
-        nc.gpsimd.memset(w4_s[:].bitcast(I32), 0)
+        nc.vector.memset(v_s1[:].bitcast(I32), 0)
+        nc.vector.memset(w4_s[:].bitcast(I32), 0)
 
         warm = held("warm", [P, 1], F32)
         warm_out = held("warm_out", [P, 1], F32)
@@ -73,7 +75,9 @@ def tile_list_glucose_hour_cells_kernel(
         gain_t = held("gain_t", [P, PACK], F32)
         base_t = held("base_t", [P, PACK], F32)
         page = [held(f"page{t}", [P, T2], F32) for t in range(PACK)]
-        wgs_t = [held(f"wgs{t}", [P, S], F32) for t in range(PACK)]
+        h = held("h", [P, PACK, S], F32)
+        wgs_last = held("wgs_last", [P, S], F32)
+        wgs_t = [h[:, t + 1, :] for t in range(PACK - 1)] + [wgs_last[:]]
         w3_raw = held("w3_raw", [P, PACK, N], F32)
         w4_w = held("w4_w", [P, N], U32)
         page0_rows = page0.rearrange("(p t) m -> p t m", t=PACK)
@@ -98,12 +102,17 @@ def tile_list_glucose_hour_cells_kernel(
             for quad in (0, 2, 1, 3):
                 nc.sync.dma_start(wgs_t[t][quad * QUAD : (quad + 1) * QUAD, :], wgs_rows[:, t, :])
 
+        load_scales(nc.gpsimd, w2_s_raw, w2_scales)
+        load_scales(nc.gpsimd, w4_s, w4_scales)
         nc.sync.dma_start(w2_w_raw[:].bitcast(I32), w2_words.rearrange("a p n -> p a n").bitcast(I32))
         nc.sync.dma_start(pick[:], offs)
         nc.sync.dma_start(put[:], offs2)
-        load_scales(nc.sync, tab_s, tab_scales)
+        for quad in (0, 2, 1, 3):
+            nc.sync.dma_start(
+                tab_s[quad * QUAD : quad * QUAD + 4 * PASSES, :].bitcast(I32),
+                tab_scales[:, 4 * quad : 4 * quad + 4, :].bitcast(I32),
+            )
         load_tab(0)
-        load_scales(nc.sync, w2_s_raw, w2_scales)
         load_w1(0)
         load_tab(1)
         load_w1(1)
@@ -115,16 +124,21 @@ def tile_list_glucose_hour_cells_kernel(
         nc.sync.dma_start(w3_raw[:], w3.rearrange("(p j) n -> p j n", j=PACK))
 
         w2_w = held("w2_w", [P, PASSES, 2 * H], U8)
-        w2_s = held("w2_s", [P, PASSES * H], U8)
+        w2_s = held("w2_s", [P, PASSES * H], U8, "tab_w0")
         for a in range(PASSES):
             nc.vector.tensor_copy(
                 w2_w[:, a, :].rearrange("p (t q b) -> p t q b", t=PACK, b=2),
                 w2_w_raw[:, a, :].rearrange("p (q t b) -> p t q b", t=PACK, b=2),
             )
-        v_s = [held(f"v_s{a}", [P, S], U8) for a in range(PASSES)]
+        v_s0 = held("v_s0", [P, S], U8)
+        v_s = [v_s0, v_s1]
         v_w = [held(f"v_w{a}", [P, S], U32) for a in range(PASSES)]
-        for a in range(PASSES):
-            nc.vector.tensor_copy(v_s[a][:], tab_s[:, a * T : (a + 1) * T].indirect(pick[:]))
+        nc.vector.tensor_copy(v_s0[:], tab_s[:].indirect(pick[:]))
+        for quad in range(4):
+            nc.scalar.dma_start(
+                v_s1[quad * QUAD : quad * QUAD + 4, :].bitcast(I32),
+                v_s0[quad * QUAD + 4 : quad * QUAD + 8, :].bitcast(I32),
+            )
         nc.vector.tensor_copy(v_w[0][:], tab_w[0][:].indirect(pick[:]))
         nc.vector.tensor_copy(
             w2_s[:].rearrange("p (a t q) -> p a t q", a=PASSES, t=PACK),
@@ -145,7 +159,6 @@ def tile_list_glucose_hour_cells_kernel(
                 nc.vector.tensor_copy(dst, src)
             nc.vector.quantize_mx(out=w1_w[a][:].bitcast(FP8X4), scales=w1_s[a][:], in_=w1_b[a][:])
 
-        h = held("h", [P, PACK, S], F32)
         x_pairs = [held(f"x_pairs{c}", [P, 2, HALF, 2], BF16, f"w1_b{c}") for c in range(HALVES)]
         y_pairs = [held(f"y_pairs{k}", [P, 2, PAGE_CHUNK, 2], BF16) for k in range(T2 // PAGE_CHUNK)]
 
@@ -181,15 +194,15 @@ def tile_list_glucose_hour_cells_kernel(
                 sq.append(work.tile([P, HALF], F32, name="sq", bufs=2))
                 nc.scalar.activation(sq[c][:], banks[c][:], ACT.Square)
             for c in range(HALVES):
-                rs.append(work.tile([P, HALF], F32, name="rs", bufs=8))
+                rs.append(work.tile([P, HALF], F32, name="rs", bufs=2))
                 nc.scalar.activation(rs[c][:], sq[c][:], ACT.Abs_reciprocal_sqrt, bias=1.0)
-            return rs
-
-        def features(t, rs):
-            rows = slice(t * P, (t + 1) * P)
-            damp = held(f"damp{t}", [P, S], F32, f"wgs{t - 1}" if t else None)
+            damp = held(f"damp{t}", [P, S], F32)
             for c in range(HALVES):
                 nc.scalar.activation(damp[:, half_cols(c)], rs[c][:], ACT.Square)
+            return damp
+
+        def features(t, damp):
+            rows = slice(t * P, (t + 1) * P)
             for c in range(HALVES):
                 a_ps = psum.tile([P, HALF], F32, name="a_bank")
                 for a in range(PASSES):
@@ -207,17 +220,21 @@ def tile_list_glucose_hour_cells_kernel(
                 )
 
         def scatter(t):
-            nc.vector.tensor_tensor(page[t][:].indirect(put[:]), h[:, t, :], wgs_t[t][:], ALU.mult)
+            nc.vector.tensor_tensor(page[t][:].indirect(put[:]), h[:, t, :], wgs_t[t], ALU.mult)
             nc.sync.dma_start(out_1_rows[:, t, :], page[t][:])
 
-        def fetch(t):
-            for c in range(HALVES):
-                round_page(t, c)
+        def fetch_half(t, c):
+            if True:
                 got = work.tile([P, HALF], F32, name="got", bufs=4)
                 nc.vector.tensor_copy(got[:], page[t][:].indirect(half_list(read, c)))
                 nc.scalar.activation(
                     x_pairs[c][:, t // 2, :, t % 2], got[:], ACT.Identity, bias=base_t[:, t : t + 1], scale=-1.0
                 )
+
+        def fetch(t):
+            for c in range(HALVES):
+                round_page(t, c)
+                fetch_half(t, c)
             for k in range(HALVES, T2 // PAGE_CHUNK):
                 round_page(t, k)
 
@@ -231,10 +248,9 @@ def tile_list_glucose_hour_cells_kernel(
             features(t + 1, roots[t + 1])
             fetch(t)
         nc.sync.dma_start(w4_w[:].bitcast(I32), w4_words[0].rearrange("p n i -> p (n i)").bitcast(I32))
-        load_scales(nc.sync, w4_s, w4_scales)
 
         w3_b = held("w3_b", [P, PACK * N], BF16)
-        w3_w = held("w3_w", [P, N], U32, "wgs2")
+        w3_w = held("w3_w", [P, N], U32, "damp3")
         w3_s = held("w3_s", [P, N], U8)
         nc.scalar.copy(weave_out(w3_b[:]), weave_in(w3_raw[:]))
         for lo, hi in ((0, 256), (256, N)):
@@ -248,9 +264,8 @@ def tile_list_glucose_hour_cells_kernel(
             nc.scalar.copy(weave_out(woven_h[c][:]), weave_in(h[:, :, half_cols(c)]))
 
         scatter(PACK - 1)
-        fetch(PACK - 1)
 
-        h_w = held("h_w", [P, S], U32, "wgs3")
+        h_w = held("h_w", [P, S], U32, "wgs_last")
         h_s = held("h_s", [P, S], U8)
         score = {}
 
@@ -277,6 +292,8 @@ def tile_list_glucose_hour_cells_kernel(
         y_s = held("y_s", [P, T2], U8)
         words_out = out_2[0].rearrange("p m i -> p (m i)").bitcast(I32)
 
+        done = []
+
         def scores(c, woven):
             nc.vector.quantize_mx(out=x_w[:, half_cols(c)].bitcast(FP8X4), scales=x_s[:, half_cols(c)], in_=woven[:])
             for nb in range(N // P):
@@ -290,29 +307,37 @@ def tile_list_glucose_hour_cells_kernel(
                     start=False,
                     stop=True,
                 )
-                y = work.tile([P, HALF], F32, name="y", tag="rs", bufs=8)
+                y = work.tile([P, HALF], F32, name="y", bufs=6)
                 nc.scalar.activation(y[:], score[c, nb][:], ACT.Copy, scale=-1.0)
-                nc.sync.dma_start(out_0[rows, half_cols(c)], y[:])
+                done.append((rows, c, y))
 
         def planes(k, woven):
             cols = slice(k * PAGE_CHUNK, (k + 1) * PAGE_CHUNK)
             nc.vector.quantize_mx(out=y_w[:, cols].bitcast(FP8X4), scales=y_s[:, cols], in_=woven[:])
             nc.sync.dma_start(words_out[:, cols], y_w[:, cols].bitcast(I32))
 
-        own_scores(0)
-        wx0 = weave_pairs(x_pairs[0], nc.vector.tensor_copy, I32)
+        round_page(3, 0)
+        fetch_half(3, 0)
+        fetch_half(3, 1)
+        round_page(3, 1)
+        round_page(3, 2)
+        round_page(3, 3)
         wy0 = weave_pairs(y_pairs[0], nc.vector.tensor_copy, I32)
-        scores(0, wx0)
+        wx0 = weave_pairs(x_pairs[0], nc.vector.tensor_copy, I32)
         planes(0, wy0)
-        own_scores(1)
+        own_scores(0)
+        scores(0, wx0)
         wx1 = weave_pairs(x_pairs[1], nc.vector.tensor_copy, I32)
-        wy1 = weave_pairs(y_pairs[1], nc.vector.tensor_copy, I32)
+        own_scores(1)
         scores(1, wx1)
-        planes(1, wy1)
+        wy1 = weave_pairs(y_pairs[1], nc.vector.tensor_copy, I32)
         wy2 = weave_pairs(y_pairs[2], nc.vector.tensor_copy, I32)
+        planes(1, wy1)
         wy3 = weave_pairs(y_pairs[3], nc.vector.tensor_copy, I32)
         planes(2, wy2)
         planes(3, wy3)
+        for rows, c, y in done:
+            nc.sync.dma_start(out_0[rows, half_cols(c)], y[:])
         for quad in range(4):
             nc.sync.dma_start(
                 out_3[0, 4 * quad : 4 * quad + 4, :].bitcast(I32), y_s[quad * QUAD : quad * QUAD + 4, :].bitcast(I32)

@@ -64,11 +64,6 @@ def tile_list_glucose_hour_cells_kernel(
         nc.vector.memset(v_s1[:].bitcast(I32), 0)
         nc.vector.memset(w4_s[:].bitcast(I32), 0)
 
-        warm = held("warm", [P, 1], F32)
-        warm_out = held("warm_out", [P, 1], F32)
-        nc.vector.memset(warm[:], 1.0)
-        nc.scalar.activation(warm_out[:], warm[:], ACT.Abs_reciprocal_sqrt)
-
         tab_w = [held(f"tab_w{a}", [P, T], U32) for a in range(PASSES)]
         w1_raw = [held(f"w1_raw{a}", [P, PACK, H], F32) for a in range(PASSES)]
         w2_w_raw = held("w2_w_raw", [P, PASSES, 2 * H], U8)
@@ -102,43 +97,44 @@ def tile_list_glucose_hour_cells_kernel(
             for quad in (0, 2, 1, 3):
                 nc.sync.dma_start(wgs_t[t][quad * QUAD : (quad + 1) * QUAD, :], wgs_rows[:, t, :])
 
-        load_scales(nc.gpsimd, w2_s_raw, w2_scales)
-        load_scales(nc.gpsimd, w4_s, w4_scales)
         nc.sync.dma_start(w2_w_raw[:].bitcast(I32), w2_words.rearrange("a p n -> p a n").bitcast(I32))
         nc.sync.dma_start(pick[:], offs)
-        nc.sync.dma_start(put[:], offs2)
         for quad in (0, 2, 1, 3):
             nc.sync.dma_start(
                 tab_s[quad * QUAD : quad * QUAD + 4 * PASSES, :].bitcast(I32),
                 tab_scales[:, 4 * quad : 4 * quad + 4, :].bitcast(I32),
             )
         load_tab(0)
-        load_w1(0)
+        load_scales(nc.sync, w2_s_raw, w2_scales)
         load_tab(1)
+        load_w1(0)
+        v_s0 = held("v_s0", [P, S], U8)
+        nc.vector.tensor_copy(v_s0[:], tab_s[:].indirect(pick[:]))
+        for quad in (0, 2, 1, 3):
+            nc.sync.dma_start(
+                v_s1[quad * QUAD : quad * QUAD + 4, :].bitcast(I32),
+                v_s0[quad * QUAD + 4 : quad * QUAD + 8, :].bitcast(I32),
+            )
         load_w1(1)
+        nc.sync.dma_start(put[:], offs2)
         nc.sync.dma_start(gain_t[:], gain.rearrange("(p t) -> p t", t=PACK))
         load_slice(0)
         nc.sync.dma_start(read[:], offs3)
         nc.sync.dma_start(base_t[:], base.rearrange("(p t) -> p t", t=PACK))
         load_slice(1)
         nc.sync.dma_start(w3_raw[:], w3.rearrange("(p j) n -> p j n", j=PACK))
+        nc.sync.dma_start(w4_w[:].bitcast(I32), w4_words[0].rearrange("p n i -> p (n i)").bitcast(I32))
+        load_scales(nc.sync, w4_s, w4_scales)
 
         w2_w = held("w2_w", [P, PASSES, 2 * H], U8)
-        w2_s = held("w2_s", [P, PASSES * H], U8, "tab_w0")
+        w2_s = held("w2_s", [P, PASSES * H], U8)
         for a in range(PASSES):
             nc.vector.tensor_copy(
                 w2_w[:, a, :].rearrange("p (t q b) -> p t q b", t=PACK, b=2),
                 w2_w_raw[:, a, :].rearrange("p (q t b) -> p t q b", t=PACK, b=2),
             )
-        v_s0 = held("v_s0", [P, S], U8)
         v_s = [v_s0, v_s1]
         v_w = [held(f"v_w{a}", [P, S], U32) for a in range(PASSES)]
-        nc.vector.tensor_copy(v_s0[:], tab_s[:].indirect(pick[:]))
-        for quad in range(4):
-            nc.scalar.dma_start(
-                v_s1[quad * QUAD : quad * QUAD + 4, :].bitcast(I32),
-                v_s0[quad * QUAD + 4 : quad * QUAD + 8, :].bitcast(I32),
-            )
         nc.vector.tensor_copy(v_w[0][:], tab_w[0][:].indirect(pick[:]))
         nc.vector.tensor_copy(
             w2_s[:].rearrange("p (a t q) -> p a t q", a=PASSES, t=PACK),
@@ -148,15 +144,13 @@ def tile_list_glucose_hour_cells_kernel(
             nc.vector.tensor_copy(v_w[1][:, half_cols(c)], tab_w[1][:].indirect(half_list(pick, c)))
 
         w1_b = [held(f"w1_b{a}", [P, PACK * H], BF16) for a in range(PASSES)]
-        w1_w = [held("w1_w0", [P, H], U32, "tab_w1"), held("w1_w1", [P, H], U32)]
         w1_s = [held(f"w1_s{a}", [P, H], U8) for a in range(PASSES)]
         for a in range(PASSES):
             dst = w1_b[a][:].rearrange("p (t q j) -> p q j t", t=PACK, j=PACK)
             src = w1_raw[a][:].rearrange("p j (q t) -> p q j t", t=PACK)
-            if a == 0:
-                nc.scalar.copy(dst, src)
-            else:
-                nc.vector.tensor_copy(dst, src)
+            nc.vector.tensor_copy(dst, src)
+        w1_w = [held("w1_w0", [P, H], U32, "w1_raw1"), held("w1_w1", [P, H], U32)]
+        for a in range(PASSES):
             nc.vector.quantize_mx(out=w1_w[a][:].bitcast(FP8X4), scales=w1_s[a][:], in_=w1_b[a][:])
 
         x_pairs = [held(f"x_pairs{c}", [P, 2, HALF, 2], BF16, f"w1_b{c}") for c in range(HALVES)]
@@ -168,8 +162,8 @@ def tile_list_glucose_hour_cells_kernel(
         def weave_pairs(pairs, copy, word):
             woven = work.tile([P, PACK * HALF], BF16, name="woven", bufs=5, align_bytes=64)
             copy(
-                woven[:].bitcast(word).rearrange("p (c i u) -> p c u i", i=4, u=2),
-                pairs[:].rearrange("p u m e -> p u (m e)").bitcast(word).rearrange("p u (c i) -> p c u i", i=4),
+                woven[:].bitcast(word).rearrange("p (m u) -> p m u", u=2),
+                pairs[:].rearrange("p u m e -> p u (m e)").bitcast(word).rearrange("p u m -> p m u"),
             )
             return woven
 
@@ -178,7 +172,7 @@ def tile_list_glucose_hour_cells_kernel(
         def root(t):
             banks, sq, rs = [], [], []
             for c in range(HALVES):
-                b_ps = psum.tile([P, HALF], F32, name="b_bank")
+                b_ps = psum.tile([P, HALF], F32, name="b_bank", bufs=6)
                 for a in range(PASSES):
                     nc.tensor.matmul_mx(
                         out=b_ps[:],
@@ -201,10 +195,12 @@ def tile_list_glucose_hour_cells_kernel(
                 nc.scalar.activation(damp[:, half_cols(c)], rs[c][:], ACT.Square)
             return damp
 
+        gained = {t: held(f"gained{t}", [P, S], F32) for t in range(1, PACK)}
+
         def features(t, damp):
             rows = slice(t * P, (t + 1) * P)
             for c in range(HALVES):
-                a_ps = psum.tile([P, HALF], F32, name="a_bank")
+                a_ps = psum.tile([P, HALF], F32, name="a_bank", bufs=2)
                 for a in range(PASSES):
                     nc.tensor.matmul_mx(
                         out=a_ps[:],
@@ -215,9 +211,12 @@ def tile_list_glucose_hour_cells_kernel(
                         start=(a == 0),
                         stop=(a == PASSES - 1),
                     )
-                nc.vector.scalar_tensor_tensor(
-                    h[:, t, half_cols(c)], a_ps[:], gain_t[:, t : t + 1], damp[:, half_cols(c)], ALU.mult, ALU.mult
-                )
+                if t == 0:
+                    nc.vector.scalar_tensor_tensor(
+                        h[:, t, half_cols(c)], a_ps[:], gain_t[:, t : t + 1], damp[:, half_cols(c)], ALU.mult, ALU.mult
+                    )
+                else:
+                    nc.scalar.activation(gained[t][:, half_cols(c)], a_ps[:], ACT.Copy, scale=gain_t[:, t : t + 1])
 
         def scatter(t):
             nc.vector.tensor_tensor(page[t][:].indirect(put[:]), h[:, t, :], wgs_t[t], ALU.mult)
@@ -240,14 +239,15 @@ def tile_list_glucose_hour_cells_kernel(
 
         roots = [root(0)]
         features(0, roots[0])
-        roots.extend(root(t) for t in range(1, PACK))
+        for t in range(1, PACK):
+            roots.append(root(t))
+            features(t, roots[t])
         for t in range(PACK - 1):
             scatter(t)
             if t + 2 < PACK:
                 load_slice(t + 2)
-            features(t + 1, roots[t + 1])
+            nc.gpsimd.tensor_tensor(h[:, t + 1, :], gained[t + 1][:], roots[t + 1][:], ALU.mult)
             fetch(t)
-        nc.sync.dma_start(w4_w[:].bitcast(I32), w4_words[0].rearrange("p n i -> p (n i)").bitcast(I32))
 
         w3_b = held("w3_b", [P, PACK * N], BF16)
         w3_w = held("w3_w", [P, N], U32, "damp3")
@@ -275,7 +275,7 @@ def tile_list_glucose_hour_cells_kernel(
             )
             for nb in range(N // P):
                 rows = slice(nb * P, (nb + 1) * P)
-                score[c, nb] = psum.tile([P, HALF], F32, name=("a_bank", "b_bank")[c])
+                score[c, nb] = psum.tile([P, HALF], F32, name="b_bank", bufs=6)
                 nc.tensor.matmul_mx(
                     out=score[c, nb][:],
                     lhsT=w4_w[:, rows].bitcast(FP8X4),

from contextlib import ExitStack

import concourse.mybir as mybir

K, T, S, H, T2, N = 1024, 2048, 1024, 512, 2048, 384
FLOPS = 2 * (2 * K * H * S + 2 * H * N * S)

F32 = mybir.dt.float32
BF16 = mybir.dt.bfloat16
I32 = mybir.dt.int32
U32 = mybir.dt.uint32
U16 = mybir.dt.uint16
U8 = mybir.dt.uint8
FP8X4 = mybir.dt.float8_e4m3fn_x4
FP4X4 = mybir.dt.float4_e2m1fn_x4
ACT = mybir.ActivationFunctionType
ALU = mybir.AluOpType

P = 128
PACK = 4
QUAD = 32
PASSES = K // (P * PACK)
HALF = 512
HALVES = S // HALF
LIST_COLS = S // 16
PAGE_CHUNK = 512


def tile_list_glucose_hour_cells_kernel(
    tc, tab_words, tab_scales, offs, offs2, offs3, w1, w2_words, w2_scales, gain, page0, wgs, base, w3,
    w4_words, w4_scales, out_0, out_1, out_2, out_3,
):
    nc = tc.nc
    with ExitStack() as ctx:
        keep = ctx.enter_context(tc.tile_pool(name="keep", bufs=1))
        work = ctx.enter_context(tc.tile_pool(name="work", bufs=4))
        psum = ctx.enter_context(tc.psum_pool(name="psum", bufs=4))

        def held(name, shape, dtype, tag=None):
            return keep.tile(shape, dtype, name=name, tag=tag or name, align_bytes=64)

        def half_cols(c):
            return slice(c * HALF, (c + 1) * HALF)

        def half_list(lst, c):
            return lst[:, c * HALF // 16 : (c + 1) * HALF // 16]

        def weave_out(flat):
            return flat.rearrange("p (c i t) -> p c t i", i=4, t=PACK)

        def weave_in(rows):
            return rows.rearrange("p t (c i) -> p c t i", i=4)

        pick = keep.tile([P, LIST_COLS], U16, name="pick")
        put = keep.tile([P, LIST_COLS], U16, name="put")
        read = keep.tile([P, LIST_COLS], U16, name="read")

        tab_s = held("tab_s", [P, T], U8)
        v_s1 = held("v_s1", [P, S], U8)
        w2_s_raw = held("w2_s_raw", [P, PASSES * H], U8)
        w4_s = held("w4_s", [P, N], U8)
        nc.vector.memset(tab_s[:].bitcast(I32), 0)
        nc.gpsimd.memset(w2_s_raw[:].bitcast(I32), 0)
        nc.vector.memset(v_s1[:].bitcast(I32), 0)
        nc.vector.memset(w4_s[:].bitcast(I32), 0)

        tab_w = [held(f"tab_w{a}", [P, T], U32) for a in range(PASSES)]
        w1_raw = [held(f"w1_raw{a}", [P, PACK, H], F32) for a in range(PASSES)]
        w2_w_raw = held("w2_w_raw", [P, PASSES, 2 * H], U8)
        gain_t = held("gain_t", [P, PACK], F32)
        base_t = held("base_t", [P, PACK], F32)
        page = [held(f"page{t}", [P, T2], F32) for t in range(PACK)]
        h = held("h", [P, PACK, S], F32)
        wgs_last = held("wgs_last", [P, S], F32)
        wgs_t = [h[:, t + 1, :] for t in range(PACK - 1)] + [wgs_last[:]]
        w3_raw = held("w3_raw", [P, PACK, N], F32)
        w4_w = held("w4_w", [P, N], U32)
        page0_rows = page0.rearrange("(p t) m -> p t m", t=PACK)
        wgs_rows = wgs.rearrange("(q t) s -> q t s", t=PACK)

        def load_tab(a):
            nc.sync.dma_start(tab_w[a][:].bitcast(I32), tab_words[a].rearrange("p n i -> p (n i)").bitcast(I32))

        def load_w1(a):
            rows = w1[a * P * PACK : (a + 1) * P * PACK, :]
            nc.sync.dma_start(w1_raw[a][:], rows.rearrange("(p j) c -> p j c", j=PACK))

        def load_scales(queue, plane, scales):
            for quad in (0, 2, 1, 3):
                queue.dma_start(
                    plane[quad * QUAD : quad * QUAD + 4, :].bitcast(I32).rearrange("r (a n) -> r a n", a=scales.shape[0]),
                    scales[:, 4 * quad : 4 * quad + 4, :].rearrange("a r n -> r a n").bitcast(I32),
                )

        def load_slice(t):
            nc.sync.dma_start(page[t][:], page0_rows[:, t, :])
            for quad in (0, 2, 1, 3):
                nc.sync.dma_start(wgs_t[t][quad * QUAD : (quad + 1) * QUAD, :], wgs_rows[:, t, :])

        nc.sync.dma_start(w2_w_raw[:].bitcast(I32), w2_words.rearrange("a p n -> p a n").bitcast(I32))
        nc.sync.dma_start(pick[:], offs)
        for quad in (0, 2, 1, 3):
            nc.sync.dma_start(
                tab_s[quad * QUAD : quad * QUAD + 4 * PASSES, :].bitcast(I32),
                tab_scales[:, 4 * quad : 4 * quad + 4, :].bitcast(I32),
            )
        load_tab(0)
        load_scales(nc.sync, w2_s_raw, w2_scales)
        load_tab(1)
        load_w1(0)
        v_s0 = held("v_s0", [P, S], U8)
        nc.vector.tensor_copy(v_s0[:], tab_s[:].indirect(pick[:]))
        for quad in (0, 2, 1, 3):
            nc.sync.dma_start(
                v_s1[quad * QUAD : quad * QUAD + 4, :].bitcast(I32),
                v_s0[quad * QUAD + 4 : quad * QUAD + 8, :].bitcast(I32),
            )
        load_w1(1)
        nc.sync.dma_start(put[:], offs2)
        nc.sync.dma_start(gain_t[:], gain.rearrange("(p t) -> p t", t=PACK))
        load_slice(0)
        nc.sync.dma_start(read[:], offs3)
        nc.sync.dma_start(base_t[:], base.rearrange("(p t) -> p t", t=PACK))
        load_slice(1)
        nc.sync.dma_start(w3_raw[:], w3.rearrange("(p j) n -> p j n", j=PACK))
        nc.sync.dma_start(w4_w[:].bitcast(I32), w4_words[0].rearrange("p n i -> p (n i)").bitcast(I32))
        load_scales(nc.sync, w4_s, w4_scales)

        w2_w = held("w2_w", [P, PASSES, 2 * H], U8)
        w2_s = held("w2_s", [P, PASSES * H], U8)
        for a in range(PASSES):
            nc.vector.tensor_copy(
                w2_w[:, a, :].rearrange("p (t q b) -> p t q b", t=PACK, b=2),
                w2_w_raw[:, a, :].rearrange("p (q t b) -> p t q b", t=PACK, b=2),
            )
        v_s = [v_s0, v_s1]
        v_w = [held(f"v_w{a}", [P, S], U32) for a in range(PASSES)]
        nc.vector.tensor_copy(v_w[0][:], tab_w[0][:].indirect(pick[:]))
        nc.vector.tensor_copy(
            w2_s[:].rearrange("p (a t q) -> p a t q", a=PASSES, t=PACK),
            w2_s_raw[:].rearrange("p (a q t) -> p a t q", a=PASSES, t=PACK),
        )
        for c in range(HALVES):
            nc.vector.tensor_copy(v_w[1][:, half_cols(c)], tab_w[1][:].indirect(half_list(pick, c)))

        w1_b = [held(f"w1_b{a}", [P, PACK * H], BF16) for a in range(PASSES)]
        w1_s = [held(f"w1_s{a}", [P, H], U8) for a in range(PASSES)]
        for a in range(PASSES):
            dst = w1_b[a][:].rearrange("p (t q j) -> p q j t", t=PACK, j=PACK)
            src = w1_raw[a][:].rearrange("p j (q t) -> p q j t", t=PACK)
            nc.vector.tensor_copy(dst, src)
        w1_w = [held("w1_w0", [P, H], U32, "w1_raw1"), held("w1_w1", [P, H], U32)]
        for a in range(PASSES):
            nc.vector.quantize_mx(out=w1_w[a][:].bitcast(FP8X4), scales=w1_s[a][:], in_=w1_b[a][:])

        x_pairs = [held(f"x_pairs{c}", [P, 2, HALF, 2], BF16, f"w1_b{c}") for c in range(HALVES)]
        y_pairs = [held(f"y_pairs{k}", [P, 2, PAGE_CHUNK, 2], BF16) for k in range(T2 // PAGE_CHUNK)]

        def round_page(t, k):
            nc.scalar.copy(y_pairs[k][:, t // 2, :, t % 2], page[t][:, k * PAGE_CHUNK : (k + 1) * PAGE_CHUNK])

        def weave_pairs(pairs, copy, word):
            woven = work.tile([P, PACK * HALF], BF16, name="woven", bufs=5, align_bytes=64)
            copy(
                woven[:].bitcast(word).rearrange("p (m u) -> p m u", u=2),
                pairs[:].rearrange("p u m e -> p u (m e)").bitcast(word).rearrange("p u m -> p m u"),
            )
            return woven

        out_1_rows = out_1.rearrange("(p t) m -> p t m", t=PACK)

        def root(t):
            banks, sq, rs = [], [], []
            for c in range(HALVES):
                b_ps = psum.tile([P, HALF], F32, name="b_bank", bufs=6)
                for a in range(PASSES):
                    nc.tensor.matmul_mx(
                        out=b_ps[:],
                        lhsT=w2_w[:, a, 2 * t * P : 2 * (t + 1) * P].bitcast(FP4X4),
                        lhsT_scale=w2_s[:, a * H + t * P : a * H + (t + 1) * P],
                        rhs=v_w[a][:, half_cols(c)].bitcast(FP8X4),
                        rhs_scale=v_s[a][:, half_cols(c)],
                        start=(a == 0),
                        stop=(a == PASSES - 1),
                    )
                banks.append(b_ps)
            for c in range(HALVES):
                sq.append(work.tile([P, HALF], F32, name="sq", bufs=2))
                nc.scalar.activation(sq[c][:], banks[c][:], ACT.Square)
            for c in range(HALVES):
                rs.append(work.tile([P, HALF], F32, name="rs", bufs=2))
                nc.scalar.activation(rs[c][:], sq[c][:], ACT.Abs_reciprocal_sqrt, bias=1.0)
            damp = held(f"damp{t}", [P, S], F32)
            for c in range(HALVES):
                nc.scalar.activation(damp[:, half_cols(c)], rs[c][:], ACT.Square)
            return damp

        gained = {t: held(f"gained{t}", [P, S], F32) for t in range(1, PACK)}

        def features(t, damp):
            rows = slice(t * P, (t + 1) * P)
            for c in range(HALVES):
                a_ps = psum.tile([P, HALF], F32, name="a_bank", bufs=2)
                for a in range(PASSES):
                    nc.tensor.matmul_mx(
                        out=a_ps[:],
                        lhsT=w1_w[a][:, rows].bitcast(FP8X4),
                        lhsT_scale=w1_s[a][:, rows],
                        rhs=v_w[a][:, half_cols(c)].bitcast(FP8X4),
                        rhs_scale=v_s[a][:, half_cols(c)],
                        start=(a == 0),
                        stop=(a == PASSES - 1),
                    )
                if t == 0:
                    nc.vector.scalar_tensor_tensor(
                        h[:, t, half_cols(c)], a_ps[:], gain_t[:, t : t + 1], damp[:, half_cols(c)], ALU.mult, ALU.mult
                    )
                else:
                    nc.scalar.activation(gained[t][:, half_cols(c)], a_ps[:], ACT.Copy, scale=gain_t[:, t : t + 1])

        def scatter(t):
            nc.vector.tensor_tensor(page[t][:].indirect(put[:]), h[:, t, :], wgs_t[t], ALU.mult)
            nc.sync.dma_start(out_1_rows[:, t, :], page[t][:])

        def fetch_half(t, c):
            if True:
                got = work.tile([P, HALF], F32, name="got", bufs=4)
                nc.vector.tensor_copy(got[:], page[t][:].indirect(half_list(read, c)))
                nc.scalar.activation(
                    x_pairs[c][:, t // 2, :, t % 2], got[:], ACT.Identity, bias=base_t[:, t : t + 1], scale=-1.0
                )

        def fetch(t):
            for c in range(HALVES):
                round_page(t, c)
                fetch_half(t, c)
            for k in range(HALVES, T2 // PAGE_CHUNK):
                round_page(t, k)

        roots = [root(0)]
        features(0, roots[0])
        for t in range(1, PACK):
            roots.append(root(t))
            features(t, roots[t])
        for t in range(PACK - 1):
            scatter(t)
            if t + 2 < PACK:
                load_slice(t + 2)
            nc.gpsimd.tensor_tensor(h[:, t + 1, :], gained[t + 1][:], roots[t + 1][:], ALU.mult)
            fetch(t)

        w3_b = held("w3_b", [P, PACK * N], BF16)
        w3_w = held("w3_w", [P, N], U32, "damp3")
        w3_s = held("w3_s", [P, N], U8)
        nc.scalar.copy(weave_out(w3_b[:]), weave_in(w3_raw[:]))
        for lo, hi in ((0, 256), (256, N)):
            nc.vector.quantize_mx(
                out=w3_w[:, lo:hi].bitcast(FP8X4), scales=w3_s[:, lo:hi], in_=w3_b[:, PACK * lo : PACK * hi]
            )

        woven_h = []
        for c in range(HALVES):
            woven_h.append(work.tile([P, PACK * HALF], BF16, name="woven", bufs=5, align_bytes=64))
            nc.scalar.copy(weave_out(woven_h[c][:]), weave_in(h[:, :, half_cols(c)]))

        scatter(PACK - 1)

        h_w = held("h_w", [P, S], U32, "wgs_last")
        h_s = held("h_s", [P, S], U8)
        score = {}

        def own_scores(c):
            nc.vector.quantize_mx(
                out=h_w[:, half_cols(c)].bitcast(FP8X4), scales=h_s[:, half_cols(c)], in_=woven_h[c][:]
            )
            for nb in range(N // P):
                rows = slice(nb * P, (nb + 1) * P)
                score[c, nb] = psum.tile([P, HALF], F32, name="b_bank", bufs=6)
                nc.tensor.matmul_mx(
                    out=score[c, nb][:],
                    lhsT=w4_w[:, rows].bitcast(FP8X4),
                    lhsT_scale=w4_s[:, rows],
                    rhs=h_w[:, half_cols(c)].bitcast(FP8X4),
                    rhs_scale=h_s[:, half_cols(c)],
                    start=True,
                    stop=False,
                )

        x_w = held("x_w", [P, S], U32, "tab_w1")
        x_s = held("x_s", [P, S], U8)
        y_w = held("y_w", [P, T2], U32, "tab_w0")
        y_s = held("y_s", [P, T2], U8)
        words_out = out_2[0].rearrange("p m i -> p (m i)").bitcast(I32)

        done = []

        def scores(c, woven):
            nc.vector.quantize_mx(out=x_w[:, half_cols(c)].bitcast(FP8X4), scales=x_s[:, half_cols(c)], in_=woven[:])
            for nb in range(N // P):
                rows = slice(nb * P, (nb + 1) * P)
                nc.tensor.matmul_mx(
                    out=score[c, nb][:],
                    lhsT=w3_w[:, rows].bitcast(FP8X4),
                    lhsT_scale=w3_s[:, rows],
                    rhs=x_w[:, half_cols(c)].bitcast(FP8X4),
                    rhs_scale=x_s[:, half_cols(c)],
                    start=False,
                    stop=True,
                )
                y = work.tile([P, HALF], F32, name="y", bufs=6)
                nc.scalar.activation(y[:], score[c, nb][:], ACT.Copy, scale=-1.0)
                done.append((rows, c, y))

        def planes(k, woven):
            cols = slice(k * PAGE_CHUNK, (k + 1) * PAGE_CHUNK)
            nc.vector.quantize_mx(out=y_w[:, cols].bitcast(FP8X4), scales=y_s[:, cols], in_=woven[:])
            nc.sync.dma_start(words_out[:, cols], y_w[:, cols].bitcast(I32))

        round_page(3, 0)
        fetch_half(3, 0)
        fetch_half(3, 1)
        round_page(3, 1)
        round_page(3, 2)
        round_page(3, 3)
        wy0 = weave_pairs(y_pairs[0], nc.vector.tensor_copy, I32)
        wx0 = weave_pairs(x_pairs[0], nc.vector.tensor_copy, I32)
        planes(0, wy0)
        own_scores(0)
        scores(0, wx0)
        wx1 = weave_pairs(x_pairs[1], nc.vector.tensor_copy, I32)
        own_scores(1)
        scores(1, wx1)
        wy1 = weave_pairs(y_pairs[1], nc.vector.tensor_copy, I32)
        wy2 = weave_pairs(y_pairs[2], nc.vector.tensor_copy, I32)
        planes(1, wy1)
        wy3 = weave_pairs(y_pairs[3], nc.vector.tensor_copy, I32)
        planes(2, wy2)
        planes(3, wy3)
        for rows, c, y in done:
            nc.sync.dma_start(out_0[rows, half_cols(c)], y[:])
        for quad in range(4):
            nc.sync.dma_start(
                out_3[0, 4 * quad : 4 * quad + 4, :].bitcast(I32), y_s[quad * QUAD : quad * QUAD + 4, :].bitcast(I32)
            )
